import numpy as np, ml_dtypes
CORES = [26,28,98,100,106,108,122,124]
N = 8
import mx_ref
NC, G = 128, 2
C, C2 = np.float32(0.041), np.float32(0.0145)
BF = ml_dtypes.bfloat16
def cut(t, i, w=512):
    return t[:, w * i:w * i + w]
def tile(rs):
    return np.stack(rs, axis=2).reshape(128, -1).astype(BF)
def layer(w, X):
    out = []
    for i in range(G):
        for t in range(len(X)):
            p = mx_ref.matmul(mx_ref.quantize(cut(w, len(X) * i + t)), X[t])
            z = p if t == 0 else z + p
        out.append(z)
    return out
def act(Z):
    return [np.maximum(s * z, 0) * C for z in Z for s in (1, -1)]
def act2(Z):
    return [np.maximum(s * z, 0) * C2 for z in Z for s in (1, -1)]
def setup_inputs(rng):
    def f(*shape):
        return mx_ref.flush((rng.standard_normal(shape, dtype=np.float32) * np.exp2(rng.integers(-2, 3, shape[:-1] + (1,)))).astype(BF))
    return {"x": f(N, 128, 4 * NC), "w1": f(N, 128, G * 512), "w2": f(N, 128, G * 512), "w3": f(N, 128, G * 512)}
def setup_inputs_blocks(rng):
    d = setup_inputs(rng)
    for k in ("x", "w1", "w2", "w3"): d[k] = mx_ref.spread(d[k], rng, 2)
    return d
def setup_inputs_wide(rng):
    d = setup_inputs(rng)
    for k in ("x", "w1", "w2", "w3"): d[k] = mx_ref.flush((d[k].astype(np.float32) * np.exp2(rng.integers(-4, 5, (N, 1, 1))).astype(np.float32)).astype(BF))
    return d
def reference(x, w1, w2, w3, own=None):
    X = [mx_ref.quantize(x[j]) for j in range(N)]
    t = np.stack([np.stack([tile(act(layer(w1[r], [X[c]]))) for c in range(N)]) for r in range(N)])
    uset = t if own is None else own["t"]
    h = np.zeros((N, 128, 4 * NC), BF)
    for c in range(N):
        for r in range(N):
            P = layer(w2[r], [mx_ref.quantize(uset[r][c])])
            Z = P if r == 0 else [z + p for z, p in zip(Z, P)]
        h[c] = tile(act2(Z))
    use = h if own is None else own["h"]
    H = [mx_ref.quantize(use[j]) for j in range(N)]
    y = np.zeros((N, 128, N * G * NC), np.float32)
    for r in range(N):
        for j in range(N):
            Z = layer(w3[r], [H[j]])
            for i in range(G):
                y[r][:, NC * (G * j + i):NC * (G * j + i) + NC] = Z[i]
    return {"t": t, "h": h, "y": y}

import numpy as np
from concourse.bass import DstId, RemoteDMATransfer
from concourse.mybir import dt, AluOpType, ActivationFunctionType

C1 = float(np.float32(0.041))
C2 = float(np.float32(0.0145))
NC = 128
U8 = "uint8"
MX = "float8_e4m3fn_x4"

SCRATCH = {
    "xs": ("sbuf", [128, 512], "bfloat16"),
    "w1s": ("sbuf", [128, 1024], "bfloat16"),
    "w2s": ("sbuf", [128, 1024], "bfloat16"),
    "w3s": ("sbuf", [128, 1024], "bfloat16"),
    "w1q": ("sbuf", [128, 256], MX), "w1p": ("sbuf", [128, 256], U8),
    "w2q": ("sbuf", [128, 256], MX), "w2p": ("sbuf", [128, 256], U8),
    "w3q": ("sbuf", [128, 256], MX), "w3p": ("sbuf", [128, 256], U8),
    "v2q": ("sbuf", [128, 256], MX), "v2p": ("sbuf", [128, 256], U8),
    "xq": ("sbuf", [128, 1024], MX), "xp": ("sbuf", [128, 1024], U8),
    "tb": ("sbuf", [128, 4096], "bfloat16"),
    "tq": ("sbuf", [128, 1024], MX), "tp": ("sbuf", [128, 1024], U8),
    "uq": ("sbuf", [128, 1024], MX), "up": ("sbuf", [128, 1024], U8),
    "pf": ("sbuf", [128, 768], "float32"),
    "la": ("sbuf", [128, 768], "float32"),
    "rl": ("sbuf", [128, 768], "float32"),
    "acc": ("sbuf", [128, 256], "float32"),
    "hb": ("sbuf", [128, 512], "bfloat16"),
    "hq": ("sbuf", [128, 1024], MX), "hp": ("sbuf", [128, 1024], U8),
    "yb": ("sbuf", [128, 2048], "float32"),
    "ps": ("psum", [128, 4096], "float32"),
}
SEMAPHORES = (["ldx", "ld1", "ld2", "ld3", "qx", "q1", "q2", "q3", "snt", "snf", "snh", "sn2", "st", "w2a", "hS", "hV", "hqd"]
              + ["%s%d" % (n, i) for n in ("xa0", "xa1", "ha0", "ha1") for i in range(8)]
              + ["%s%d" % (n, i) for n in ("za", "zb", "tS", "tV", "tqd", "ya", "yb", "yc") for i in range(8)]
              + ["%s%d" % (n, i) for n in ("pa", "pr", "pc", "pd", "pe", "ta", "ad") for i in range(4)])

CFG = {
    "both": ("h", "h"),
    "whelp": (True, True),
    "nhelp": 3,
    "lonefirst": True,
    "pord": (0, 1),
    "fwdmask": {"": "all"},
    "w2mask": "on", "tmask": "all",
    "nb": {"": (3,), "wt": (2, 1)}, "hb": {"": (1, 1, 1)}, "look": {"": 2},
    "tg": {"": ((0, 4),), "wt": ((0, 3), (3, 1))},
    "ynb": {"": (3,), "wt": (2, 1)}, "yhb": {"": (1, 1, 1)},
    "sord": "t0 t1 |snf tN tH |snh h y0 y1 yN yH",
}


def ne(mask):
    return bin(mask).count("1")


def make_plan(cores, topo, ph):
    chips = []
    for c in cores:
        if topo.chip(c) not in chips:
            chips.append(topo.chip(c))
    pair = {}
    for p in chips:
        a, b = [c for c in cores if topo.chip(c) == p]
        if not all(topo.may_write(a, d) for d in cores if d != a):
            a, b = b, a
        pair[p] = (a, b)
    wide = [p for p in chips if any(topo.same_plane(p, q) for q in chips)]
    lone = [p for p in chips if p not in wide]
    both = CFG["both"][ph]
    slots, hand, first, idx, helper, role = {}, {}, {}, {}, {}, {}
    rings = {}
    for p in chips:
        a, b = pair[p]
        others = [q for q in chips if q != p]
        if p in wide:
            k = wide.index(p)
            ring = rings[p] = [wide[(k + 1 + i) % len(wide)] for i in range(len(wide) - 1)]
            hl = [a, pair[ring[0]][1]] + [pair[q][0] for q in lone] + [pair[q][1] for q in lone]
            ht = [b] + [pair[q][0] for q in ring] + [pair[q][1] for q in ring[1:]]
            idx[p] = {q: i for i, q in enumerate(ring + lone)}
            role[a], role[b] = "wl", "wt"
        else:
            hl = [a] + [pair[q][1] for q in others]
            ht = [b] + [pair[q][0] for q in others]
            idx[p] = {q: i for i, q in enumerate(others)}
            role[a], role[b] = "ll", "lt"
        hs = [c for c in range(max(cores) + 8) if topo.chip(c) == p and c not in cores
              and all(topo.may_write(c, pair[q][0]) for q in others)]
        hs = [c for c in hs if topo.die(c) == topo.die(b)] + [c for c in hs if topo.die(c) != topo.die(b)]
        helper[p] = {q: hs[min(i, CFG["nhelp"] - 1)] for i, q in enumerate(others)}
        slots[p] = {c: i for i, c in enumerate(hl + ht)}
        hand[a], hand[b] = hl, ht
        for c in cores:
            if topo.chip(c) != p:
                first[(p, c)] = b if c in hl else a

    def other(c):
        a, b = pair[topo.chip(c)]
        return b if c == a else a

    def klass(q, c):
        l = topo.chip(c) in lone
        if c == pair[topo.chip(c)][0]:
            return "L" if l else "l"
        return "h" if l else "r" if q in lone else "t"

    def dsts_of(qs, c):
        one = [first[(q, c)] for q in qs]
        two = [other(first[(q, c)]) for q in qs if klass(q, c) in both]
        return one + two
    own, relay, fwd = [], [], []
    for p in chips:
        a, b = pair[p]
        if p in wide:
            ring = rings[p]
            wh = CFG["whelp"][ph]
            own.append((a, (a,), [b] + dsts_of((lone + ring) if CFG["lonefirst"] else (ring + lone), a)))
            own.append((b, (b,), ([helper[p][lone[0]]] if wh else []) + [a] + dsts_of(ring, b)))
            relay.append((helper[p][lone[0]] if wh else a, (b,), dsts_of(lone, b)))
        else:
            others = [q for q in chips if q != p]
            hq = []
            for q in others:
                if helper[p][q] not in hq:
                    hq.append(helper[p][q])
            own.append((a, (a,), [b] + dsts_of(others, a)))
            own.append((b, (b,), hq + [a]))
            for h in hq:
                relay.append((h, (b,), dsts_of([q for q in others if helper[p][q] == h], b)))
        for r, n in ((a, hand[b][1:]), (b, hand[a][1:])):
            runs, prev = [], False
            for c in n:
                if klass(p, c) in both:
                    prev = False
                    continue
                if prev and klass(p, c) != "h":
                    runs[-1].append(c)
                else:
                    runs.append([c])
                prev = True
            for run in runs:
                fwd.append((r, tuple(run), [other(r)]))
    return {"pair": pair, "slots": slots, "hand": hand, "first": first, "idx": idx, "helper": helper,
            "own": own, "relay": relay, "fwd": fwd, "role": role,
            "active": [mv[0] for mv in relay]}


def rank_program(g, core, T, topo):
    cores = list(T.cores)
    PL = {"xa": make_plan(cores, topo, 0), "ha": make_plan(cores, topo, 1)}
    P = PL["xa"]
    chip = topo.chip(core)
    rank = T.rank_of(core)
    if rank is None and core not in P["active"] + PL["ha"]["active"]:
        return
    S = T.sem
    sent = {"snt": 0, "snf": 0, "snh": 0, "sn2": 0}
    OFF = topo.mask(core, [c for c in cores if topo.chip(c) != chip][0])
    ALL = topo.mask(core, [c for c in cores if topo.chip(c) == chip and c != core][0])
    MK = {"all": ALL, "on": ALL & ~OFF, "off": OFF}
    TM, WM = MK[CFG["tmask"]], MK[CFG["w2mask"]]
    add, mult, mx = AluOpType.add, AluOpType.mult, AluOpType.max
    Relu, Copy = ActivationFunctionType.Relu, ActivationFunctionType.Copy

    def did(d):
        rid, pid, _ = topo.addr(d)
        return DstId(rid=rid, pnc=pid)

    def slot(c, tile):
        return P["slots"][topo.chip(c)][tile]

    def masks(src, dsts):
        here = topo.chip(src)
        offd = [d for d in dsts if topo.chip(d) != here]
        ond = [d for d in dsts if topo.chip(d) == here]
        off_m = topo.mask(src, [c for c in cores if topo.chip(c) != here][0])
        on_m = topo.mask(src, [c for c in cores if topo.chip(c) == here and c != src][0])
        if not offd:
            fm = CFG["fwdmask"].get(P["role"].get(src), CFG["fwdmask"][""])
            return [(ond, on_m if fm == "all" else on_m & ~off_m)]
        if not ond:
            return [(offd, off_m)]
        return [(ond, on_m & ~off_m), (offd, off_m)]

    arr = {}
    for pre in ("xa", "ha"):
        for kind in ("own", "relay", "fwd"):
            for src, tiles, dsts in PL[pre][kind]:
                for ds, m in masks(src, dsts):
                    for d in ds:
                        for tl in tiles:
                            arr[(pre, d, tl)] = (cores.index(tiles[0]), ne(m))

    def wait_tile(q, pre, tiles, parts=(0, 1)):
        seen = []
        for tl in tiles:
            if (pre, core, tl) in arr:
                k = arr[(pre, core, tl)]
                if k not in seen:
                    seen.append(k)
                    for w in parts:
                        q.wait_ge(S["%s%d%d" % (pre, w, k[0])], k[1])

    def move(mv, pre, cq, cp, ls="snt", wait=False):
        src, tiles, dsts = mv
        n = NC * len(tiles)
        a = NC * min(slot(core, tl) for tl in tiles)
        for which in CFG["pord"]:
            trs = []
            if wait:
                wait_tile(g, pre, tiles, (which,))
            for ds, m in masks(src, dsts):
                dst = []
                for d in ds:
                    b = NC * min(slot(d, tl) for tl in tiles)
                    dst.append(cq[:, b:b + n].bitcast(dt.uint8) if which == 0 else cp[:, b:b + n])
                srcv = cq[:, a:a + n].bitcast(dt.uint8) if which == 0 else cp[:, a:a + n]
                trs.append(RemoteDMATransfer(dst_ids=[did(d) for d in ds], dma_engine_mask=m,
                                             remote_sem=S["%s%d%d" % (pre, which, cores.index(tiles[0]))], srcs=[srcv], dsts=dst))
                sent[ls] += ne(m)
            g.remote_dma_fused(trs, local_sem=S[ls])

    def push(out, in_, d, sem, m, ls="snt"):
        rid, pid, _ = topo.addr(d)
        g.remote_dma(out, in_, sem, S[ls], pid, rid, m)
        sent[ls] += ne(m)

    if rank is None:
        b = P["pair"][chip][1]
        for pre, cq, cp in (("xa", T.xq, T.xp), ("ha", T.hq, T.hp)):
            if pre == "ha" and P["role"][b] == "lt":
                for j, d in enumerate(P["hand"][b][1:]):
                    if P["helper"][chip][topo.chip(d)] != core:
                        continue
                    g.wait_ge(S["pr%d" % j], ne(ALL))
                    k = P["idx"][topo.chip(d)][chip]
                    push(T.la[:, 256 * k:256 * k + 256], T.rl[:, 256 * j:256 * j + 256], d, S["pa%d" % k], OFF)
            for mv in PL[pre]["relay"]:
                if mv[0] == core:
                    move(mv, pre, cq, cp, "snt", True)
        g.wait_ge(S.snt, sent["snt"])
        return

    def cf(name, c=core):
        v = CFG[name]
        return v.get(P["role"][c], v[""])
    lead, trail = P["pair"][chip]
    partner = trail if core == lead else lead
    mine = P["hand"][core]
    so, sp = slot(core, core), slot(core, partner)
    ks = P["slots"][chip]
    at = {i: c for c, i in ks.items()}

    def runs(lo, sizes):
        out = []
        for m in sizes:
            out.append((lo, m))
            lo += m
        return out
    hbs = runs(so + 1, cf("hb"))
    batches = [(so, 1), (sp, 1)] + runs(sp + 1, cf("nb")) + hbs
    nk, nh = len(batches), len(hbs)
    k0 = nk - nh
    nyn = len(cf("ynb"))
    ybs = [(so, 1), (sp, 1)] + runs(sp + 1, cf("ynb")) + runs(so + 1, cf("yhb"))
    look = cf("look")

    def tiles_of(bt):
        return [at[s] for s in range(bt[0], bt[0] + bt[1])]

    def batch_of(s):
        return [k for k, (lo, m) in enumerate(batches) if lo <= s < lo + m][0]
    tg = cf("tg")
    tgp = cf("tg", partner)

    def ta_of(s):
        return [i for i, (lo, m) in enumerate(tgp) if so + lo <= s < so + lo + m][0]

    te, sc, ve, y = g.tensor, g.scalar, g.vector, g.sync

    def bank(b, n, lo=0):
        return T.ps[:, 512 * b + lo:512 * b + lo + n]

    def prod(b, n, terms, sem):
        for i, (wq, wp, wi, mq, mp, c0) in enumerate(terms):
            ins = te.matmul_mx(bank(b, n), wq[:, 128 * wi:128 * wi + 128], wp[:, 128 * wi:128 * wi + 128],
                               mq[:, c0:c0 + n], mp[:, c0:c0 + n], i == 0, i == len(terms) - 1)
        ins.then_inc(sem, 1)

    y.dma_start(T.xs[:], T.x[:]).then_inc(S.ldx, 16)
    y.dma_start(T.w1s[:], T.w1[:]).then_inc(S.ld1, 16)
    y.dma_start(T.w2s[:], T.w2[:]).then_inc(S.ld2, 16)
    y.dma_start(T.w3s[:], T.w3[:]).then_inc(S.ld3, 16)
    ve.wait_ge(S.ldx, 16)
    ve.quantize_mx(T.xq[:, NC * so:NC * so + NC], T.xp[:, NC * so:NC * so + NC], T.xs[:]).then_inc(S.qx, 1)
    ve.wait_ge(S.ld1, 16)
    ve.quantize_mx(T.w1q[:], T.w1p[:], T.w1s[:]).then_inc(S.q1, 1)
    ve.wait_ge(S.ld2, 16)
    ve.quantize_mx(T.w2q[:], T.w2p[:], T.w2s[:]).then_inc(S.q2, 1)
    te.wait_ge(S.qx, 1)
    te.wait_ge(S.q1, 1)

    def first_layer(k):
        lo, m = batches[k]
        zb = 2 * (k % 2)
        wait_tile(te, "xa", tiles_of(batches[k]))
        if k >= 2:
            te.wait_ge(S["tS%d" % (k - 2)], 2)
            te.wait_ge(S["tV%d" % (k - 2)], 2)
        for i, nm in ((0, "za"), (1, "zb")):
            prod(zb + i, NC * m, [(T.w1q, T.w1p, i, T.xq, T.xp, NC * lo)], S["%s%d" % (nm, k)])
        sc.wait_ge(S["za%d" % k], 1)
        for b, f in ((0, C1), (1, -C1)):
            sc.activation(T.tb[:, 512 * lo + b:512 * (lo + m):4], bank(zb, NC * m), Relu, scale=f).then_inc(S["tS%d" % k], 1)
        ve.wait_ge(S["zb%d" % k], 1)
        for b, f in ((2, C1), (3, -C1)):
            ve.tensor_scalar(T.tb[:, 512 * lo + b:512 * (lo + m):4], bank(zb + 1, NC * m), f, 0.0, mult, mx).then_inc(S["tV%d" % k], 1)
        ve.wait_ge(S["tS%d" % k], 2)
        ve.wait_ge(S["tV%d" % k], 2)
        ve.quantize_mx(T.tq[:, NC * lo:NC * (lo + m)], T.tp[:, NC * lo:NC * (lo + m)], T.tb[:, 512 * lo:512 * (lo + m)]).then_inc(S["tqd%d" % k], 1)

    def terms(i, lo):
        return [(T.v2q, T.v2p, i, T.uq, T.up, NC * lo), (T.w2q, T.w2p, i, T.tq, T.tp, NC * lo)]
    seen_ta = []

    def wait_ta(lo, m):
        for s in range(lo, lo + m):
            i = ta_of(s)
            if i not in seen_ta:
                seen_ta.append(i)
                te.wait_ge(S["ta%d" % i], 2 * ne(TM))

    def free_bank(j):
        if j >= 2:
            l2, m2 = hbs[j - 2]
            for s in range(l2, l2 + m2):
                te.wait_ge(S["pc%d" % (s - so - 1)], 2)

    def second_layer(j):
        lo, m = hbs[j]
        pb = 4 + 2 * (j % 2)
        wait_ta(lo, m)
        te.wait_ge(S["tqd%d" % (k0 + j)], 1)
        free_bank(j)
        for i, nm in ((0, "pd"), (1, "pe")):
            prod(pb + i, NC * m, terms(i, lo), S["%s%d" % (nm, j)])
        sc.wait_ge(S["pd%d" % j], 1)
        ve.wait_ge(S["pe%d" % j], 1)
        for s in range(lo, lo + m):
            q, c = s - so - 1, 256 * (s - so - 1)
            sc.activation(T.pf[:, c:c + 128], bank(pb, NC, NC * (s - lo)), Copy).then_inc(S["pc%d" % q], 1)
            ve.tensor_copy(T.pf[:, c + 128:c + 256], bank(pb + 1, NC, NC * (s - lo))).then_inc(S["pc%d" % q], 1)

    for k in range(k0):
        first_layer(k)
        if k == 1:
            ve.wait_ge(S.ld3, 16)
            ve.quantize_mx(T.w3q[:], T.w3p[:], T.w3s[:]).then_inc(S.q3, 1)
    te.wait_ge(S.q2, 1)
    te.wait_ge(S.w2a, 2 * ne(WM))
    for j in range(nh + look):
        if j < nh:
            first_layer(k0 + j)
        if look <= j:
            second_layer(j - look)
    wait_ta(so, 1)
    te.wait_ge(S.tqd0, 1)
    pb = 4 + 2 * (nh % 2)
    free_bank(nh)
    for i, nm in ((0, "pd"), (1, "pe")):
        prod(pb + i, NC, terms(i, so), S["%s%d" % (nm, nh)])

    ve.wait_ge(S["pd%d" % nh], 1)
    ve.wait_ge(S["pe%d" % nh], 1)
    ve.wait_ge(S.pa0, ne(OFF))
    for i in (0, 1):
        ve.tensor_tensor(T.acc[:, 128 * i:128 * i + 128], bank(pb + i, NC), T.la[:, 128 * i:128 * i + 128], add).then_inc(S.ad0, 1)
    ve.wait_ge(S.ad0, 2)
    ve.wait_ge(S.pa1, ne(OFF))
    ve.tensor_tensor(T.acc[:], T.acc[:], T.la[:, 256:512], add).then_inc(S.ad1, 1)
    ve.wait_ge(S.ad1, 1)
    ve.wait_ge(S.pa2, ne(OFF))
    for i in (0, 1):
        ve.tensor_tensor(T.acc[:, 128 * i:128 * i + 128], T.acc[:, 128 * i:128 * i + 128],
                         T.la[:, 512 + 128 * i:512 + 128 * i + 128], add).then_inc(S["ad%d" % (2 + i)], 1)
    sc.wait_ge(S.ad2, 1)
    for b, f in ((0, C2), (1, -C2)):
        sc.activation(T.hb[:, b:512:4], T.acc[:, 0:128], Relu, scale=f).then_inc(S.hS, 1)
    sc.wait_ge(S.ad3, 1)
    sc.activation(T.hb[:, 2:512:4], T.acc[:, 128:256], Relu, scale=C2).then_inc(S.hS, 1)
    ve.wait_ge(S.ad3, 1)
    ve.tensor_scalar(T.hb[:, 3:512:4], T.acc[:, 128:256], -C2, 0.0, mult, mx).then_inc(S.hV, 1)
    ve.wait_ge(S.hV, 1)
    ve.wait_ge(S.hS, 3)
    ve.quantize_mx(T.hq[:, NC * so:NC * so + NC], T.hp[:, NC * so:NC * so + NC], T.hb[:]).then_inc(S.hqd, 1)

    te.wait_ge(S.q3, 1)
    te.wait_ge(S.hqd, 1)
    for k, bt in enumerate(ybs):
        b0 = (2 * k) % 8
        wait_tile(te, "ha", tiles_of(bt))
        if k >= 4:
            te.wait_ge(S["yc%d" % (k - 4)], 2 * ybs[k - 4][1])
        for i, nm in ((0, "ya"), (1, "yb")):
            prod(b0 + i, NC * bt[1], [(T.w3q, T.w3p, i, T.hq, T.hp, NC * bt[0])], S["%s%d" % (nm, k)])
        sc.wait_ge(S["ya%d" % k], 1)
        ve.wait_ge(S["yb%d" % k], 1)
        for j, tl in enumerate(tiles_of(bt)):
            c = 256 * cores.index(tl)
            sc.activation(T.yb[:, c:c + 128], bank(b0, NC, NC * j), Copy).then_inc(S["yc%d" % k], 1)
            ve.tensor_copy(T.yb[:, c + 128:c + 256], bank(b0 + 1, NC, NC * j)).then_inc(S["yc%d" % k], 1)

    def gather(pre, cq, cp, ls, ls2, between):
        for mv in PL[pre]["own"]:
            if mv[0] == core:
                move(mv, pre, cq, cp, ls)
        between()
        for kind in ("relay", "fwd"):
            for mv in PL[pre][kind]:
                if mv[0] == core:
                    move(mv, pre, cq, cp, ls2, True)

    def send_w2():
        g.wait_ge(S.q2, 1)
        push(T.v2q[:].bitcast(dt.uint8), T.w2q[:].bitcast(dt.uint8), partner, S.w2a, WM)
        push(T.v2p[:], T.w2p[:], partner, S.w2a, WM)

    g.wait_ge(S.qx, 1)
    gather("xa", T.xq, T.xp, "snt", "snt", send_w2)
    for gi, (lo, m) in enumerate(tg):
        for kb in sorted(set(batch_of(sp + lo + i) for i in range(m))):
            g.wait_ge(S["tqd%d" % kb], 1)
        a, b = NC * (sp + lo), NC * (sp + lo + m)
        push(T.uq[:, a:b].bitcast(dt.uint8), T.tq[:, a:b].bitcast(dt.uint8), partner, S["ta%d" % gi], TM)
        push(T.up[:, a:b], T.tp[:, a:b], partner, S["ta%d" % gi], TM)
    for j, d in enumerate(mine[1:]):
        g.wait_ge(S["pc%d" % j], 2)
        k = P["idx"][topo.chip(d)][chip]
        if topo.may_write(core, d):
            push(T.la[:, 256 * k:256 * k + 256], T.pf[:, 256 * j:256 * j + 256], d, S["pa%d" % k], OFF, "snf")
        else:
            push(T.rl[:, 256 * j:256 * j + 256], T.pf[:, 256 * j:256 * j + 256], P["helper"][chip][topo.chip(d)], S["pr%d" % j], ALL, "snf")
    g.wait_ge(S.hqd, 1)
    gather("ha", T.hq, T.hp, "snh", "sn2", lambda: None)
    for ls in ("snt", "snf", "snh", "sn2"):
        g.wait_ge(S[ls], sent[ls])

    nst = [0]

    def store(out, in_):
        y.dma_start(out, in_).then_inc(S.st, 16)
        nst[0] += 16

    def tstore(k):
        y.wait_ge(S["tqd%d" % k], 1)
        for tl in tiles_of(batches[k]):
            s = ks[tl]
            store(T.t[cores.index(tl)], T.tb[:, 512 * s:512 * s + 512])

    def ystore(k):
        y.wait_ge(S["yc%d" % k], 2 * ybs[k][1])
        rs = sorted(cores.index(tl) for tl in tiles_of(ybs[k]))
        while rs:
            m = 1
            while m < len(rs) and rs[m] == rs[0] + m:
                m += 1
            a, b = 256 * rs[0], 256 * (rs[0] + m)
            store(T.y[:, a:b], T.yb[:, a:b])
            rs = rs[m:]
    tk = {"t0": [0], "t1": [1], "tN": range(2, k0), "tH": range(k0, nk)}
    yk = {"y0": [0], "y1": [1], "yN": range(2, 2 + nyn), "yH": range(2 + nyn, len(ybs))}
    for tok in CFG["sord"].split():
        if tok[0] == "|":
            y.wait_ge(S[tok[1:]], sent[tok[1:]])
        elif tok == "h":
            y.wait_ge(S.hqd, 1)
            store(T.h[:], T.hb[:])
        elif tok in tk:
            for k in tk[tok]:
                tstore(k)
        else:
            for k in yk[tok]:
                ystore(k)
    y.wait_ge(S.st, nst[0])
